import numpy as np
import ml_dtypes


def mxq(x, axis, fmt="e4m3"):
    dtype, down = {"e4m3": (ml_dtypes.float8_e4m3fn, 7), "e5m2": (ml_dtypes.float8_e5m2, 14)}[fmt]
    v = np.moveaxis(np.asarray(x, np.float32).astype(ml_dtypes.bfloat16).astype(np.float64), axis, -1)
    blocks = v.reshape(v.shape[:-1] + (-1, 32))
    amax = np.abs(blocks).max(-1, keepdims=True)
    byte = np.maximum(np.where(amax > 0, np.frexp(amax)[1] - 1 + 127, 0) - down, 1)
    scale = np.exp2(byte - 127.0)
    codes = (blocks / scale).astype(np.float32).astype(dtype).astype(np.float64)
    return np.moveaxis((codes * scale).reshape(v.shape), -1, axis)


WIDE = False


def mx_kscale(k):
    if not WIDE:
        return np.ones(k)
    levels = np.array([10, -10, 5, -5, 0])
    if k % 512:
        return np.exp2(np.random.permutation(np.resize(levels, k // 32))).repeat(32)
    a = np.empty((k // 512, 16))
    for p in range(k // 512):
        a[p, :8] = np.random.permutation(np.resize(levels, 8))
        for g in range(8):
            far = levels[np.abs(levels - a[p, g]) >= 10]
            a[p, g + 8] = far[np.random.randint(len(far))]
    return np.exp2(a.ravel()).repeat(32)


def f64(x):
    return np.asarray(x).astype(np.float64)


def striped(idx):
    return np.tile(idx.reshape(-1, 16).T, (8, 1)).astype(np.uint16)


def unstriped(offs):
    return offs[:16].T.reshape(-1).astype(np.int64)


def striped8(idx):
    return np.concatenate([x.reshape(-1, 16).T for x in idx]).astype(np.uint16)


def runs(offs, k):
    lists = np.stack([offs[16 * r : 16 * r + 16].T.reshape(-1) for r in range(8)]).astype(np.int64)
    return lists[np.arange(k) % 512 // 64]


def pack_weight(w):
    k, n = w.shape
    w = f64(np.asarray(w, np.float32).astype(ml_dtypes.bfloat16)).reshape(k // 32, 32, n)
    amax = np.abs(w).max(1)
    byte = np.clip(np.where(amax > 0, np.frexp(amax)[1] - 1 + 127 - 7, 1), 1, 254)
    scaled = (w * np.exp2(127.0 - byte)[:, None, :]).reshape(k, n).astype(np.float32)
    words = np.ascontiguousarray(scaled.reshape(k // 512, 128, 4, n).transpose(0, 1, 3, 2)).astype(ml_dtypes.float8_e4m3fn).view(np.uint8)
    return words, np.ascontiguousarray(byte.astype(np.uint8).reshape(k // 512, 16, n))


def unpack_weight(words, scales):
    g, p, n, _ = words.shape
    vals = np.ascontiguousarray(words).view(ml_dtypes.float8_e4m3fn).astype(np.float64) * np.repeat(np.exp2(scales.astype(np.float64) - 127.0), 8, axis=1)[..., None]
    return vals.transpose(0, 1, 3, 2).reshape(g * 512, n)

def planes(y):
    n, m = y.shape
    v = y.astype(np.float32).astype(ml_dtypes.bfloat16).astype(np.float64).reshape(n // 32, 32, m)
    top = np.abs(v).max(1)
    byte = np.clip(np.where(top > 0, np.frexp(top)[1] - 1 + 127 - 7, 1), 1, 254)
    codes = (v * np.exp2(127.0 - byte)[:, None, :]).reshape(n, m).astype(np.float32).astype(ml_dtypes.float8_e4m3fn).view(np.uint8)
    words = codes.reshape(n // 512, 128, 4, m).transpose(0, 1, 3, 2)
    return np.ascontiguousarray(words), np.ascontiguousarray(byte.astype(np.uint8).reshape(n // 512, 16, m))


K, T, S, N, H, W = 512, 2048, 512, 512, 512, 2048


def setup_inputs():
    n = np.random.standard_normal
    s = mx_kscale(K)[:, None]
    u = mx_kscale(H)
    packed_xT = pack_weight(n((K, T)) * s)
    packed_w1 = pack_weight(n((K, H)) / np.sqrt(K) / s)
    packed_w2 = pack_weight(n((H, N)) / np.sqrt(2 * H) / u[:, None])
    packed_w3 = pack_weight(n((K, N)) / np.sqrt(2 * K) / s)
    return {
        "x_words": packed_xT[0],
        "x_scales": packed_xT[1],
        "w1_words": packed_w1[0],
        "w1_scales": packed_w1[1],
        "gn": (np.random.uniform(0.5, 1.5, (H, 1)) * u[:, None]).astype(np.float32),
        "w2_words": packed_w2[0],
        "w2_scales": packed_w2[1],
        "w3_words": packed_w3[0],
        "w3_scales": packed_w3[1],
        "offs": striped(np.random.permutation(T)[:S]),
        "n1": striped(np.random.randint(0, S, W)),
        "hz": striped8(np.random.randint(0, T, (8, S))),
        "n2": striped8(np.stack([np.random.permutation(S) for _ in range(8)])),
        "n3": striped8(np.stack([np.random.permutation(S) for _ in range(8)])),
    }


def reference(x_words, x_scales, w1_words, w1_scales, gn, w2_words, w2_scales, w3_words, w3_scales, offs, n1, hz, n2, n3):
    xq = unpack_weight(x_words, x_scales)[:, unstriped(offs)]
    y = unpack_weight(w1_words, w1_scales).T @ xq
    mb = y[:, unstriped(n1)]
    mx = mb.reshape(H, S, 4).max(axis=2)
    mn = mb.reshape(H, S, 4).min(axis=2)
    z = f64(gn) * (mx - (0.5 * mn))
    x_hz = unpack_weight(x_words, x_scales)[np.arange(K)[:, None], runs(hz, K)]
    h = unpack_weight(w2_words, w2_scales).T @ mxq(z, 0, "e4m3") + unpack_weight(w3_words, w3_scales).T @ x_hz
    out_0 = (h - (h[np.arange(N)[:, None], runs(n2, N)])) / (np.abs(h[np.arange(N)[:, None], runs(n3, N)] - h) + 0.5)
    return (out_0,) + planes(out_0)

@@ -1,0 +1,325 @@
+from contextlib import ExitStack
+
+import concourse.mybir as mybir
+
+K, T, S, N, H, W = 512, 2048, 512, 512, 512, 2048
+FLOPS = 3 * 2 * 512 * 512 * 512
+
+F32 = mybir.dt.float32
+BF16 = mybir.dt.bfloat16
+I32 = mybir.dt.int32
+U32 = mybir.dt.uint32
+U16 = mybir.dt.uint16
+U8 = mybir.dt.uint8
+FP8X4 = mybir.dt.float8_e4m3fn_x4
+ALU = mybir.AluOpType
+ACT = mybir.ActivationFunctionType
+
+P = 128
+PACK = 4
+GROUP = 4
+ZC = 128
+NZ = S // ZC
+SPARE = 16
+Z_CHUNKS = ((0, 128), (128, 128), (256, 128), (384, 64), (448, 64))
+OUT_CHUNKS = ((0, 256), (256, 128), (384, 128))
+
+
+def words_view(ap):
+    return ap[0].rearrange("p n t -> p (n t)").bitcast(I32)
+
+
+def tile_picked_mixhgspanfrac_none_po_kernel(
+    tc, x_words, x_scales, w1_words, w1_scales, gn, w2_words, w2_scales, w3_words, w3_scales, offs, n1, hz, n2, n3, out_0, out_1, out_2
+):
+    nc = tc.nc
+    with ExitStack() as ctx:
+        lists = ctx.enter_context(tc.tile_pool(name="lists", bufs=1))
+        keep = ctx.enter_context(tc.tile_pool(name="keep", bufs=1))
+        psum = ctx.enter_context(tc.psum_pool(name="psum", bufs=1))
+
+        def tile(name, shape, dtype):
+            return keep.tile(shape, dtype, name=name, align_bytes=64)
+
+        offs_t = lists.tile([P, S // 16], U16, name="offs_t")
+        n1_t = lists.tile([P, W // 16], U16, name="n1_t")
+        hz_t = lists.tile([P, S // 16], U16, name="hz_t")
+        n2_t = lists.tile([P, S // 16], U16, name="n2_t")
+        n3_t = lists.tile([P, S // 16], U16, name="n3_t")
+
+        x_w = tile("x_w", [P, T], I32)
+        x_s = tile("x_s", [P, T], U8)
+        x_s_runs = tile("x_s_runs", [P, T], U8)
+        w1_w_raw = keep.tile([P, H], I32, name="w1_w_raw", tag="raw_words", align_bytes=64)
+        w1_s_raw = tile("w1_s_raw", [P, H], U8)
+        w23_s_raw = tile("w23_s_raw", [P, N], U8)
+        hz_s = tile("hz_s", [P, S], U8)
+        gain = tile("gain", [P, PACK], F32)
+        y_win = [tile(f"y_win{t}", [P, S + SPARE], F32) for t in range(PACK)]
+
+        def load_scales(queues, dst, first, src):
+            for q, queue in enumerate(queues):
+                queue.dma_start(dst[32 * q + first : 32 * q + first + 4, :].bitcast(I32), src[0, 4 * q : 4 * q + 4, :].bitcast(I32))
+
+        nc.vector.memset(w1_s_raw[:].bitcast(I32), 0)
+        nc.vector.memset(x_s[:].bitcast(I32), 0)
+        nc.sync.dma_start(offs_t[:], offs)
+        nc.scalar.dma_start(w1_w_raw[:], words_view(w1_words))
+        nc.sync.dma_start(n1_t[:], n1)
+        nc.scalar.dma_start(gain[:], gn.rearrange("(p t) o -> p (t o)", t=PACK))
+        nc.sync.dma_start(hz_t[:], hz)
+        nc.sync.dma_start(x_w[:], words_view(x_words))
+        nc.sync.dma_start(n3_t[:], n3)
+        nc.sync.dma_start(n2_t[:], n2)
+        load_scales([nc.scalar] * 4, x_s, 0, x_scales)
+        load_scales([nc.gpsimd] * 3 + [nc.scalar], w1_s_raw, 0, w1_scales)
+        nc.vector.memset(x_s_runs[:].bitcast(I32), 0)
+        nc.vector.memset(w23_s_raw[:].bitcast(I32), 0)
+        nc.vector.memset(hz_s[:].bitcast(I32), 0)
+        for t in range(PACK):
+            nc.vector.memset(y_win[t][:, S:], 0.0)
+        nc.sync.dma_start(x_s_runs[0:P:8, :].bitcast(I32), x_scales[0].bitcast(I32))
+        load_scales([nc.sync] * 4, w23_s_raw, 0, w2_scales)
+        load_scales([nc.sync] * 4, w23_s_raw, 4, w3_scales)
+
+        def deal_words(dst, src):
+            nc.vector.tensor_copy(
+                dst.rearrange("p (t a i) -> p a t i", t=PACK, i=4),
+                src.rearrange("p (a i t) -> p a t i", t=PACK, i=4),
+            )
+
+        def deal_scales(dst, src):
+            nc.vector.tensor_copy(dst.rearrange("p (t m) -> p t m", t=PACK), src.rearrange("p (m t) -> p t m", t=PACK))
+
+        w1_w = tile("w1_w", [P, H], I32)
+        w1_s = tile("w1_s", [P, H], U8)
+        deal_words(w1_w[:], w1_w_raw[:])
+        w23_w_raw = keep.tile([P, 2, N], I32, name="w23_w_raw", tag="raw_words", align_bytes=64)
+        nc.sync.dma_start(w23_w_raw[:, 0, :], words_view(w2_words))
+        nc.sync.dma_start(w23_w_raw[:, 1, :], words_view(w3_words))
+        pick_s = tile("pick_s", [P, S], U8)
+        nc.vector.tensor_copy(pick_s[:], x_s[:].indirect(offs_t[:]))
+        deal_scales(w1_s[:], w1_s_raw[:])
+
+        pick_w = tile("pick_w", [P, S], I32)
+        nc.vector.tensor_copy(pick_w[:].bitcast(U32), x_w[:].bitcast(U32).indirect(offs_t[:]))
+
+        gain_abs = tile("gain_abs", [P, PACK], F32)
+        gain_pos = tile("gain_pos", [P, PACK], F32)
+        gain_sign = tile("gain_sign", [P, PACK], BF16)
+        nc.vector.scalar_tensor_tensor(gain_abs[:], gain[:], -1.0, gain[:], ALU.mult, ALU.max)
+        nc.vector.tensor_scalar(gain_pos[:], gain[:], 0.0, 2.0, ALU.is_ge, ALU.mult)
+        nc.vector.tensor_scalar(gain_sign[:], gain_pos[:], -1.0, None, ALU.add)
+
+        y_bank = [psum.tile([P, S], F32, name=f"y_bank{t}", tag=f"bank{t}") for t in range(PACK)]
+        for t in range(PACK):
+            cols = slice(t * P, (t + 1) * P)
+            nc.tensor.matmul_mx(
+                out=y_bank[t][:],
+                lhsT=w1_w[:, cols].bitcast(FP8X4),
+                lhsT_scale=w1_s[:, cols],
+                rhs=pick_w[:].bitcast(FP8X4),
+                rhs_scale=pick_s[:],
+                start=True,
+                stop=True,
+            )
+
+        nch = len(Z_CHUNKS)
+        members = [tile(f"members{c}", [P, PACK, w * GROUP], F32) for c, (c0, w) in enumerate(Z_CHUNKS)]
+
+        def fetch_members(c, t):
+            c0, w = Z_CHUNKS[c]
+            entries = n1_t[:, c0 * GROUP // 16 : (c0 + w) * GROUP // 16]
+            nc.scalar.activation(members[c][:, t, :], y_win[t][:].indirect(entries), ACT.Copy)
+
+        def y_out_scalar(t):
+            nc.scalar.activation(y_win[t][:, :S], y_bank[t][:], ACT.Copy, scale=gain_abs[:, t : t + 1])
+
+        def y_out_vector(t):
+            nc.vector.tensor_scalar(y_win[t][:, :S], y_bank[t][:], gain_abs[:, t : t + 1], None, ALU.mult)
+
+        hz_w = tile("hz_w", [P, S], I32)
+        hz_s_runs = tile("hz_s_runs", [P, S], U8)
+        y_out_scalar(0)
+        nc.vector.tensor_copy(hz_w[:].bitcast(U32), x_w[:].bitcast(U32).indirect(hz_t[:]))
+        y_out_vector(1)
+        fetch_members(0, 0)
+        fetch_members(0, 1)
+        y_out_scalar(2)
+        y_out_vector(3)
+        nc.vector.tensor_copy(hz_s_runs[:], x_s_runs[:].indirect(hz_t[:]))
+        for r in range(4):
+            nc.sync.dma_start(hz_s[r:P:32, :].bitcast(I32), hz_s_runs[8 * r : P : 32, :].bitcast(I32))
+
+        w23_w = tile("w23_w", [P, 2, N], I32)
+        w23_s = tile("w23_s", [P, N], U8)
+
+        hi2 = [tile(f"hi2_{c}", [P, w, PACK, 2], F32) for c, (c0, w) in enumerate(Z_CHUNKS)]
+        lo2 = [tile(f"lo2_{c}", [P, w, PACK, 2], F32) for c, (c0, w) in enumerate(Z_CHUNKS)]
+        hi = [tile(f"hi_{c}", [P, w, PACK], F32) for c, (c0, w) in enumerate(Z_CHUNKS)]
+        lo = [tile(f"lo_{c}", [P, w, PACK], F32) for c, (c0, w) in enumerate(Z_CHUNKS)]
+        z_abs = [tile(f"z_abs{c}", [P, w, PACK], BF16) for c, (c0, w) in enumerate(Z_CHUNKS)]
+        z = [tile(f"z{c}", [P, w, PACK], BF16) for c, (c0, w) in enumerate(Z_CHUNKS)]
+        z_w = tile("z_w", [P, S], I32)
+        z_s = tile("z_s", [P, S], U8)
+        h_win = [tile(f"h_win{t}", [P, S], F32) for t in range(PACK)]
+        h_own = [tile(f"h_own{k}", [P, PACK, w], F32) for k, (c0, w) in enumerate(OUT_CHUNKS)]
+
+        h_shared = [psum.tile([P, PACK, ZC], F32, name=f"h_bank{b}") for b in range(NZ - 1)]
+        h_last = [psum.tile([P, ZC], F32, name=f"h_last{t}", tag=f"bank{t}") for t in range(PACK)]
+
+        def h_sum(b, t):
+            return h_last[t][:] if b == NZ - 1 else h_shared[b][:, t, :]
+
+        def pairs(c, u, dst, op):
+            m = members[c][:, 2 * u : 2 * u + 2, :].rearrange("p t (j g) -> p j t g", g=GROUP)
+            nc.vector.tensor_tensor(dst[c][:, :, 2 * u : 2 * u + 2, :], m[:, :, :, 0:2], m[:, :, :, 2:4], op)
+
+        def finish(c, dst, src, op):
+            nc.vector.tensor_tensor(dst[c][:], src[c][:, :, :, 0], src[c][:, :, :, 1], op)
+
+        def combine(c):
+            nc.vector.scalar_tensor_tensor(
+                z_abs[c][:].rearrange("p j t -> p (j t)"),
+                lo[c][:].rearrange("p j t -> p (j t)"),
+                -0.5,
+                hi[c][:].rearrange("p j t -> p (j t)"),
+                ALU.mult,
+                ALU.add,
+            )
+
+        def sign(c):
+            w = Z_CHUNKS[c][1]
+            nc.vector.tensor_tensor(z[c][:], z_abs[c][:], gain_sign[:].unsqueeze(1).to_broadcast([P, w, PACK]), ALU.mult)
+
+        def h_pass(b, which, rhs, rhs_scale):
+            cols = slice(b * ZC, (b + 1) * ZC)
+            alone = b == NZ - 1
+            for t in range(PACK):
+                rows = slice(t * P, (t + 1) * P)
+                nc.tensor.matmul_mx(
+                    out=h_sum(b, t),
+                    lhsT=w23_w[:, which, rows].bitcast(FP8X4),
+                    lhsT_scale=w23_s[4 * which : P, rows],
+                    rhs=rhs[:, cols].bitcast(FP8X4),
+                    rhs_scale=rhs_scale[:, cols],
+                    start=(which == 1 and (alone or t == 0)),
+                    stop=(which == 0 and (alone or t == PACK - 1)),
+                )
+
+        def quantise_z(c):
+            c0, w = Z_CHUNKS[c]
+            nc.vector.quantize_mx(
+                out=z_w[:, c0 : c0 + w].bitcast(FP8X4), scales=z_s[:, c0 : c0 + w], in_=z[c][:].rearrange("p j t -> p (j t)")
+            )
+            if (c0 + w) % ZC == 0:
+                h_pass(c0 // ZC, 0, z_w, z_s)
+
+        for c in range(nch):
+            for t in range(PACK):
+                if (c, t) not in ((0, 0), (0, 1)):
+                    fetch_members(c, t)
+        for c in range(nch):
+            pairs(c, 0, hi2, ALU.max)
+            if c > 0:
+                combine(c - 1)
+            pairs(c, 0, lo2, ALU.min)
+            if c > 0:
+                sign(c - 1)
+            else:
+                for which in range(2):
+                    deal_words(w23_w[:, which, :], w23_w_raw[:, which, :])
+                deal_scales(w23_s[:], w23_s_raw[:])
+                for b in range(NZ):
+                    h_pass(b, 1, hz_w, hz_s)
+            pairs(c, 1, hi2, ALU.max)
+            if c > 0:
+                quantise_z(c - 1)
+            pairs(c, 1, lo2, ALU.min)
+            finish(c, lo, lo2, ALU.min)
+            finish(c, hi, hi2, ALU.max)
+        combine(nch - 1)
+        sign(nch - 1)
+        quantise_z(nch - 1)
+
+        for b in range(NZ):
+            for t in range(PACK):
+                nc.scalar.copy(h_win[t][:, b * ZC : (b + 1) * ZC], h_sum(b, t))
+            for k, (c0, w) in enumerate(OUT_CHUNKS):
+                if c0 + w == (b + 1) * ZC:
+                    for t in range(PACK):
+                        nc.sync.dma_start(h_own[k][:, t, :], h_win[t][:, c0 : c0 + w])
+
+        out_rows = out_0.rearrange("(p t) c -> p t c", t=PACK)
+        out_w = tile("out_w", [P, S], I32)
+        out_s = tile("out_s", [P, S], U8)
+
+        def per_chunk(name):
+            return [tile(f"{name}{k}", [P, PACK, w], F32) for k, (c0, w) in enumerate(OUT_CHUNKS)]
+
+        other, diff, dist, root, inv, neg_num, res = (per_chunk(name) for name in ("other", "diff", "dist", "root", "inv", "neg_num", "res"))
+        res_b = [tile(f"res_b{k}", [P, w, PACK], BF16) for k, (c0, w) in enumerate(OUT_CHUNKS)]
+
+        def halves(k):
+            return (slice(0, 2), slice(2, 4)) if k == 0 else (slice(0, 4),)
+
+        def fetch_less_own(dst, list_t, k):
+            c0, w = OUT_CHUNKS[k]
+            for t in range(PACK):
+                nc.vector.tensor_tensor(
+                    dst[k][:, t, :], h_win[t][:].indirect(list_t[:, c0 // 16 : (c0 + w) // 16]), h_own[k][:, t, :], ALU.subtract
+                )
+
+        def fetch_other(k):
+            c0, w = OUT_CHUNKS[k]
+            for t in range(PACK):
+                nc.scalar.activation(other[k][:, t, :], h_win[t][:].indirect(n3_t[:, c0 // 16 : (c0 + w) // 16]), ACT.Copy)
+
+        def less_own(k):
+            nc.vector.tensor_tensor(diff[k][:], other[k][:], h_own[k][:], ALU.subtract)
+
+        def denominators(k):
+            for ts in halves(k):
+                nc.scalar.activation(dist[k][:, ts, :], diff[k][:, ts, :], ACT.Abs)
+                nc.scalar.activation(root[k][:, ts, :], dist[k][:, ts, :], ACT.Abs_reciprocal_sqrt, bias=0.5)
+                nc.scalar.activation(inv[k][:, ts, :], root[k][:, ts, :], ACT.Square)
+
+        def quotient(k):
+            c0, w = OUT_CHUNKS[k]
+            for ts in halves(k):
+                nc.vector.scalar_tensor_tensor(res[k][:, ts, :], neg_num[k][:, ts, :], -1.0, inv[k][:, ts, :], ALU.mult, ALU.mult)
+                nc.sync.dma_start(out_rows[:, ts, c0 : c0 + w], res[k][:, ts, :])
+
+        def interleave(k, copy):
+            copy(res_b[k][:].rearrange("p (a i) t -> p a t i", i=4), res[k][:].rearrange("p t (a i) -> p a t i", i=4))
+
+        def quantise_out(k):
+            c0, w = OUT_CHUNKS[k]
+            nc.vector.quantize_mx(
+                out=out_w[:, c0 : c0 + w].bitcast(FP8X4), scales=out_s[:, c0 : c0 + w], in_=res_b[k][:].rearrange("p j t -> p (j t)")
+            )
+            nc.sync.dma_start(words_view(out_1)[:, c0 : c0 + w], out_w[:, c0 : c0 + w])
+
+        fetch_less_own(diff, n3_t, 0)
+        fetch_other(1)
+        denominators(0)
+        fetch_less_own(neg_num, n2_t, 0)
+        less_own(1)
+        fetch_other(2)
+        denominators(1)
+        fetch_less_own(neg_num, n2_t, 1)
+        less_own(2)
+        denominators(2)
+        quotient(0)
+        interleave(0, nc.scalar.copy)
+        fetch_less_own(neg_num, n2_t, 2)
+        quotient(1)
+        interleave(1, nc.scalar.copy)
+        quotient(2)
+        quantise_out(0)
+        interleave(2, nc.vector.tensor_copy)
+        quantise_out(1)
+        quantise_out(2)
+        for q in range(4):
+            queue = nc.scalar if q % 2 else nc.sync
+            queue.dma_start(out_2[0, 4 * q : 4 * q + 4, :].bitcast(I32), out_s[32 * q : 32 * q + 4, :].bitcast(I32))

@@ -48,11 +48,10 @@ def tile_picked_mixhgspanfrac_none_po_kernel(
         n3_t = lists.tile([P, S // 16], U16, name="n3_t")
 
         x_w = tile("x_w", [P, T], I32)
-        x_s = tile("x_s", [P, T], U8)
+        x_s = keep.tile([P, T], U8, name="x_s", tag="x_s_then_hz_w", align_bytes=64)
         x_s_runs = tile("x_s_runs", [P, T], U8)
         w1_w_raw = keep.tile([P, H], I32, name="w1_w_raw", tag="raw_words", align_bytes=64)
-        w1_s_raw = tile("w1_s_raw", [P, H], U8)
-        w23_s_raw = tile("w23_s_raw", [P, N], U8)
+        w1_s_raw = keep.tile([P, H], U8, name="w1_s_raw", tag="raw_scales", align_bytes=64)
         hz_s = tile("hz_s", [P, S], U8)
         gain = tile("gain", [P, PACK], F32)
         y_win = [tile(f"y_win{t}", [P, S + SPARE], F32) for t in range(PACK)]
@@ -64,23 +63,20 @@ def tile_picked_mixhgspanfrac_none_po_kernel(
         nc.vector.memset(w1_s_raw[:].bitcast(I32), 0)
         nc.vector.memset(x_s[:].bitcast(I32), 0)
         nc.sync.dma_start(offs_t[:], offs)
-        nc.scalar.dma_start(w1_w_raw[:], words_view(w1_words))
-        nc.sync.dma_start(n1_t[:], n1)
         nc.scalar.dma_start(gain[:], gn.rearrange("(p t) o -> p (t o)", t=PACK))
+        nc.sync.dma_start(n1_t[:], n1)
+        nc.scalar.dma_start(w1_w_raw[:], words_view(w1_words))
         nc.sync.dma_start(hz_t[:], hz)
-        nc.sync.dma_start(x_w[:], words_view(x_words))
         nc.sync.dma_start(n3_t[:], n3)
         nc.sync.dma_start(n2_t[:], n2)
+        nc.sync.dma_start(x_w[:], words_view(x_words))
         load_scales([nc.scalar] * 4, x_s, 0, x_scales)
-        load_scales([nc.gpsimd] * 3 + [nc.scalar], w1_s_raw, 0, w1_scales)
+        load_scales([nc.gpsimd] + [nc.scalar] * 3, w1_s_raw, 0, w1_scales)
         nc.vector.memset(x_s_runs[:].bitcast(I32), 0)
-        nc.vector.memset(w23_s_raw[:].bitcast(I32), 0)
         nc.vector.memset(hz_s[:].bitcast(I32), 0)
         for t in range(PACK):
             nc.vector.memset(y_win[t][:, S:], 0.0)
-        nc.sync.dma_start(x_s_runs[0:P:8, :].bitcast(I32), x_scales[0].bitcast(I32))
-        load_scales([nc.sync] * 4, w23_s_raw, 0, w2_scales)
-        load_scales([nc.sync] * 4, w23_s_raw, 4, w3_scales)
+        nc.gpsimd.dma_start(x_s_runs[0:P:8, :].bitcast(I32), x_scales[0].bitcast(I32))
 
         def deal_words(dst, src):
             nc.vector.tensor_copy(
@@ -97,12 +93,16 @@ def tile_picked_mixhgspanfrac_none_po_kernel(
         w23_w_raw = keep.tile([P, 2, N], I32, name="w23_w_raw", tag="raw_words", align_bytes=64)
         nc.sync.dma_start(w23_w_raw[:, 0, :], words_view(w2_words))
         nc.sync.dma_start(w23_w_raw[:, 1, :], words_view(w3_words))
-        pick_s = tile("pick_s", [P, S], U8)
-        nc.vector.tensor_copy(pick_s[:], x_s[:].indirect(offs_t[:]))
-        deal_scales(w1_s[:], w1_s_raw[:])
-
         pick_w = tile("pick_w", [P, S], I32)
         nc.vector.tensor_copy(pick_w[:].bitcast(U32), x_w[:].bitcast(U32).indirect(offs_t[:]))
+        pick_s = keep.tile([P, S], U8, name="pick_s", tag="pick_s_then_hz_s_runs", align_bytes=64)
+        nc.vector.tensor_copy(pick_s[:], x_s[:].indirect(offs_t[:]))
+        deal_scales(w1_s[:], w1_s_raw[:])
+        w23_s_raw = keep.tile([P, N], U8, name="w23_s_raw", tag="raw_scales", align_bytes=64)
+        nc.vector.memset(w23_s_raw[:].bitcast(I32), 0)
+        load_scales([nc.sync] * 4, w23_s_raw, 4, w3_scales)
+        load_scales([nc.sync] * 4, w23_s_raw, 0, w2_scales)
+
 
         gain_abs = tile("gain_abs", [P, PACK], F32)
         gain_pos = tile("gain_pos", [P, PACK], F32)
@@ -111,8 +111,9 @@ def tile_picked_mixhgspanfrac_none_po_kernel(
         nc.vector.tensor_scalar(gain_pos[:], gain[:], 0.0, 2.0, ALU.is_ge, ALU.mult)
         nc.vector.tensor_scalar(gain_sign[:], gain_pos[:], -1.0, None, ALU.add)
 
-        y_bank = [psum.tile([P, S], F32, name=f"y_bank{t}", tag=f"bank{t}") for t in range(PACK)]
-        for t in range(PACK):
+        y_bank = [psum.tile([P, S], F32, name=f"y_bank{t}", tag=f"bank{t % 3}") for t in range(PACK)]
+
+        def y_product(t):
             cols = slice(t * P, (t + 1) * P)
             nc.tensor.matmul_mx(
                 out=y_bank[t][:],
@@ -138,15 +139,20 @@ def tile_picked_mixhgspanfrac_none_po_kernel(
         def y_out_vector(t):
             nc.vector.tensor_scalar(y_win[t][:, :S], y_bank[t][:], gain_abs[:, t : t + 1], None, ALU.mult)
 
-        hz_w = tile("hz_w", [P, S], I32)
-        hz_s_runs = tile("hz_s_runs", [P, S], U8)
+        hz_w = keep.tile([P, S], I32, name="hz_w", tag="x_s_then_hz_w", align_bytes=64)
+        hz_s_runs = keep.tile([P, S], U8, name="hz_s_runs", tag="pick_s_then_hz_s_runs", align_bytes=64)
+        y_product(0)
+        y_product(1)
+        y_product(2)
         y_out_scalar(0)
         nc.vector.tensor_copy(hz_w[:].bitcast(U32), x_w[:].bitcast(U32).indirect(hz_t[:]))
         y_out_vector(1)
+        y_out_vector(2)
+        y_product(3)
         fetch_members(0, 0)
         fetch_members(0, 1)
-        y_out_scalar(2)
-        y_out_vector(3)
+        fetch_members(0, 2)
+        y_out_scalar(3)
         nc.vector.tensor_copy(hz_s_runs[:], x_s_runs[:].indirect(hz_t[:]))
         for r in range(4):
             nc.sync.dma_start(hz_s[r:P:32, :].bitcast(I32), hz_s_runs[8 * r : P : 32, :].bitcast(I32))
@@ -163,10 +169,10 @@ def tile_picked_mixhgspanfrac_none_po_kernel(
         z_w = tile("z_w", [P, S], I32)
         z_s = tile("z_s", [P, S], U8)
         h_win = [tile(f"h_win{t}", [P, S], F32) for t in range(PACK)]
-        h_own = [tile(f"h_own{k}", [P, PACK, w], F32) for k, (c0, w) in enumerate(OUT_CHUNKS)]
+        h_own = [tile(f"h_own{half}", [P, PACK, S // 2], F32) for half in range(2)]
 
         h_shared = [psum.tile([P, PACK, ZC], F32, name=f"h_bank{b}") for b in range(NZ - 1)]
-        h_last = [psum.tile([P, ZC], F32, name=f"h_last{t}", tag=f"bank{t}") for t in range(PACK)]
+        h_last = [psum.tile([P, ZC], F32, name=f"h_last{t}", tag=f"bank{(t + 1) % 4}") for t in range(PACK)]
 
         def h_sum(b, t):
             return h_last[t][:] if b == NZ - 1 else h_shared[b][:, t, :]
@@ -215,10 +221,15 @@ def tile_picked_mixhgspanfrac_none_po_kernel(
             if (c0 + w) % ZC == 0:
                 h_pass(c0 // ZC, 0, z_w, z_s)
 
-        for c in range(nch):
+        for i in range(len(Z_CHUNKS)):
             for t in range(PACK):
-                if (c, t) not in ((0, 0), (0, 1)):
-                    fetch_members(c, t)
+                if (i, t) not in ((0, 0), (0, 1), (0, 2)):
+                    fetch_members(i, t)
+        for which in range(2):
+            deal_words(w23_w[:, which, :], w23_w_raw[:, which, :])
+        deal_scales(w23_s[:], w23_s_raw[:])
+        for b in range(NZ):
+            h_pass(b, 1, hz_w, hz_s)
         for c in range(nch):
             pairs(c, 0, hi2, ALU.max)
             if c > 0:
@@ -226,12 +237,6 @@ def tile_picked_mixhgspanfrac_none_po_kernel(
             pairs(c, 0, lo2, ALU.min)
             if c > 0:
                 sign(c - 1)
-            else:
-                for which in range(2):
-                    deal_words(w23_w[:, which, :], w23_w_raw[:, which, :])
-                deal_scales(w23_s[:], w23_s_raw[:])
-                for b in range(NZ):
-                    h_pass(b, 1, hz_w, hz_s)
             pairs(c, 1, hi2, ALU.max)
             if c > 0:
                 quantise_z(c - 1)
@@ -242,13 +247,18 @@ def tile_picked_mixhgspanfrac_none_po_kernel(
         sign(nch - 1)
         quantise_z(nch - 1)
 
-        for b in range(NZ):
+        for b in range(2):
+            nc.scalar.copy(h_own[0][:, :, b * ZC : (b + 1) * ZC], h_shared[b][:])
+        for t in range(PACK):
+            nc.sync.dma_start(h_win[t][:, : S // 2], h_own[0][:, t, :])
+        for b in range(2, NZ):
             for t in range(PACK):
                 nc.scalar.copy(h_win[t][:, b * ZC : (b + 1) * ZC], h_sum(b, t))
-            for k, (c0, w) in enumerate(OUT_CHUNKS):
-                if c0 + w == (b + 1) * ZC:
-                    for t in range(PACK):
-                        nc.sync.dma_start(h_own[k][:, t, :], h_win[t][:, c0 : c0 + w])
+        for t in range(PACK):
+            nc.sync.dma_start(h_own[1][:, t, :], h_win[t][:, S // 2 :])
+
+        def own(c0, w):
+            return h_own[c0 // (S // 2)][:, :, c0 % (S // 2) : c0 % (S // 2) + w]
 
         out_rows = out_0.rearrange("(p t) c -> p t c", t=PACK)
         out_w = tile("out_w", [P, S], I32)
@@ -257,26 +267,27 @@ def tile_picked_mixhgspanfrac_none_po_kernel(
         def per_chunk(name):
             return [tile(f"{name}{k}", [P, PACK, w], F32) for k, (c0, w) in enumerate(OUT_CHUNKS)]
 
-        other, diff, dist, root, inv, neg_num, res = (per_chunk(name) for name in ("other", "diff", "dist", "root", "inv", "neg_num", "res"))
+        diff, dist, root, inv, res = (per_chunk(name) for name in ("diff", "dist", "root", "inv", "res"))
+        other = tile("other", [P, PACK, S // 2], F32)
+        neg_num = [tile(f"neg_num{half}", [P, PACK, S // 2], F32) for half in range(2)]
         res_b = [tile(f"res_b{k}", [P, w, PACK], BF16) for k, (c0, w) in enumerate(OUT_CHUNKS)]
 
         def halves(k):
             return (slice(0, 2), slice(2, 4)) if k == 0 else (slice(0, 4),)
 
-        def fetch_less_own(dst, list_t, k):
-            c0, w = OUT_CHUNKS[k]
+        def fetch_less_own(dst, list_t, c0, w):
             for t in range(PACK):
                 nc.vector.tensor_tensor(
-                    dst[k][:, t, :], h_win[t][:].indirect(list_t[:, c0 // 16 : (c0 + w) // 16]), h_own[k][:, t, :], ALU.subtract
+                    dst[:, t, :], h_win[t][:].indirect(list_t[:, c0 // 16 : (c0 + w) // 16]), own(c0, w)[:, t, :], ALU.subtract
                 )
 
-        def fetch_other(k):
-            c0, w = OUT_CHUNKS[k]
+        def fetch_other():
             for t in range(PACK):
-                nc.scalar.activation(other[k][:, t, :], h_win[t][:].indirect(n3_t[:, c0 // 16 : (c0 + w) // 16]), ACT.Copy)
+                nc.scalar.activation(other[:, t, :], h_win[t][:].indirect(n3_t[:, S // 32 :]), ACT.Copy)
 
         def less_own(k):
-            nc.vector.tensor_tensor(diff[k][:], other[k][:], h_own[k][:], ALU.subtract)
+            c0, w = OUT_CHUNKS[k]
+            nc.vector.tensor_tensor(diff[k][:], other[:, :, c0 - S // 2 : c0 - S // 2 + w], own(c0, w), ALU.subtract)
 
         def denominators(k):
             for ts in halves(k):
@@ -287,7 +298,7 @@ def tile_picked_mixhgspanfrac_none_po_kernel(
         def quotient(k):
             c0, w = OUT_CHUNKS[k]
             for ts in halves(k):
-                nc.vector.scalar_tensor_tensor(res[k][:, ts, :], neg_num[k][:, ts, :], -1.0, inv[k][:, ts, :], ALU.mult, ALU.mult)
+                nc.vector.scalar_tensor_tensor(res[k][:, ts, :], neg_num[c0 // (S // 2)][:, ts, c0 % (S // 2) : c0 % (S // 2) + w], -1.0, inv[k][:, ts, :], ALU.mult, ALU.mult)
                 nc.sync.dma_start(out_rows[:, ts, c0 : c0 + w], res[k][:, ts, :])
 
         def interleave(k, copy):
@@ -300,19 +311,17 @@ def tile_picked_mixhgspanfrac_none_po_kernel(
             )
             nc.sync.dma_start(words_view(out_1)[:, c0 : c0 + w], out_w[:, c0 : c0 + w])
 
-        fetch_less_own(diff, n3_t, 0)
-        fetch_other(1)
+        fetch_less_own(diff[0], n3_t, *OUT_CHUNKS[0])
+        fetch_other()
         denominators(0)
-        fetch_less_own(neg_num, n2_t, 0)
         less_own(1)
-        fetch_other(2)
-        denominators(1)
-        fetch_less_own(neg_num, n2_t, 1)
         less_own(2)
+        denominators(1)
         denominators(2)
+        fetch_less_own(neg_num[0], n2_t, 0, S // 2)
         quotient(0)
         interleave(0, nc.scalar.copy)
-        fetch_less_own(neg_num, n2_t, 2)
+        fetch_less_own(neg_num[1], n2_t, S // 2, S // 2)
         quotient(1)
         interleave(1, nc.scalar.copy)
         quotient(2)

@@ -21,6 +21,7 @@ GROUP = 4
 ZC = 128
 NZ = S // ZC
 SPARE = 16
+X_S_VECTOR = 1280
 Z_CHUNKS = ((0, 128), (128, 128), (256, 128), (384, 64), (448, 64))
 OUT_CHUNKS = ((0, 256), (256, 128), (384, 128))
 
@@ -48,35 +49,42 @@ def tile_picked_mixhgspanfrac_none_po_kernel(
         n3_t = lists.tile([P, S // 16], U16, name="n3_t")
 
         x_w = tile("x_w", [P, T], I32)
-        x_s = keep.tile([P, T], U8, name="x_s", tag="x_s_then_hz_w", align_bytes=64)
-        x_s_runs = tile("x_s_runs", [P, T], U8)
-        w1_w_raw = keep.tile([P, H], I32, name="w1_w_raw", tag="raw_words", align_bytes=64)
-        w1_s_raw = keep.tile([P, H], U8, name="w1_s_raw", tag="raw_scales", align_bytes=64)
-        hz_s = tile("hz_s", [P, S], U8)
+        x_s = tile("x_s", [P, T], U8)
+        w1_w_raw = tile("w1_w_raw", [P, H], I32)
         gain = tile("gain", [P, PACK], F32)
+        w1_s_raw = keep.tile([P, H], U8, name="w1_s_raw", tag="raw_scales", align_bytes=64)
+        pick_s = tile("pick_s", [P, S], U8)
+        hz_s = tile("hz_s", [P, S], U8)
         y_win = [tile(f"y_win{t}", [P, S + SPARE], F32) for t in range(PACK)]
 
         def load_scales(queues, dst, first, src):
             for q, queue in enumerate(queues):
                 queue.dma_start(dst[32 * q + first : 32 * q + first + 4, :].bitcast(I32), src[0, 4 * q : 4 * q + 4, :].bitcast(I32))
 
+        def place_scales(queue, dst, src):
+            for r in range(4):
+                queue.dma_start(dst[r:P:32, :].bitcast(I32), src[8 * r : P : 32, :].bitcast(I32))
+
+        nc.vector.memset(x_s[:, :X_S_VECTOR].bitcast(I32), 0)
+        nc.gpsimd.memset(x_s[:, X_S_VECTOR:].bitcast(I32), 0)
+        for t in range(PACK):
+            nc.gpsimd.memset(y_win[t][:, S:], 0.0)
+        nc.gpsimd.dma_start(gain[:], gn.rearrange("(p t) o -> p (t o)", t=PACK))
         nc.vector.memset(w1_s_raw[:].bitcast(I32), 0)
-        nc.vector.memset(x_s[:].bitcast(I32), 0)
         nc.sync.dma_start(offs_t[:], offs)
-        nc.scalar.dma_start(gain[:], gn.rearrange("(p t) o -> p (t o)", t=PACK))
+        nc.sync.dma_start(w1_w_raw[:], words_view(w1_words))
+        nc.sync.dma_start(x_s[0:P:8, :].bitcast(I32), x_scales[0].bitcast(I32))
         nc.sync.dma_start(n1_t[:], n1)
-        nc.scalar.dma_start(w1_w_raw[:], words_view(w1_words))
         nc.sync.dma_start(hz_t[:], hz)
         nc.sync.dma_start(n3_t[:], n3)
         nc.sync.dma_start(n2_t[:], n2)
         nc.sync.dma_start(x_w[:], words_view(x_words))
-        load_scales([nc.scalar] * 4, x_s, 0, x_scales)
-        load_scales([nc.gpsimd] + [nc.scalar] * 3, w1_s_raw, 0, w1_scales)
-        nc.vector.memset(x_s_runs[:].bitcast(I32), 0)
+        load_scales([nc.scalar] * 4, w1_s_raw, 0, w1_scales)
+        nc.vector.memset(pick_s[:].bitcast(I32), 0)
         nc.vector.memset(hz_s[:].bitcast(I32), 0)
-        for t in range(PACK):
-            nc.vector.memset(y_win[t][:, S:], 0.0)
-        nc.gpsimd.dma_start(x_s_runs[0:P:8, :].bitcast(I32), x_scales[0].bitcast(I32))
+
+        warm = tile("warm", [P, 1], F32)
+        nc.scalar.activation(warm[:], y_win[0][:, S : S + 1], ACT.Abs_reciprocal_sqrt, bias=0.5)
 
         def deal_words(dst, src):
             nc.vector.tensor_copy(
@@ -90,18 +98,22 @@ def tile_picked_mixhgspanfrac_none_po_kernel(
         w1_w = tile("w1_w", [P, H], I32)
         w1_s = tile("w1_s", [P, H], U8)
         deal_words(w1_w[:], w1_w_raw[:])
-        w23_w_raw = keep.tile([P, 2, N], I32, name="w23_w_raw", tag="raw_words", align_bytes=64)
-        nc.sync.dma_start(w23_w_raw[:, 0, :], words_view(w2_words))
-        nc.sync.dma_start(w23_w_raw[:, 1, :], words_view(w3_words))
+        pick_s_runs = keep.tile([P, S], U8, name="pick_s_runs", tag="pick_s_runs_then_w23", align_bytes=64)
+        nc.vector.tensor_copy(pick_s_runs[:], x_s[:].indirect(offs_t[:]))
+        place_scales(nc.scalar, pick_s, pick_s_runs)
+        deal_scales(w1_s[:], w1_s_raw[:])
         pick_w = tile("pick_w", [P, S], I32)
         nc.vector.tensor_copy(pick_w[:].bitcast(U32), x_w[:].bitcast(U32).indirect(offs_t[:]))
-        pick_s = keep.tile([P, S], U8, name="pick_s", tag="pick_s_then_hz_s_runs", align_bytes=64)
-        nc.vector.tensor_copy(pick_s[:], x_s[:].indirect(offs_t[:]))
-        deal_scales(w1_s[:], w1_s_raw[:])
+        hz_s_runs = tile("hz_s_runs", [P, S], U8)
+        nc.vector.tensor_copy(hz_s_runs[:], x_s[:].indirect(hz_t[:]))
+        w23_w_raw = keep.tile([P, 2, N], I32, name="w23_w_raw", tag="pick_s_runs_then_w23", align_bytes=64)
+        nc.sync.dma_start(w23_w_raw[:, 0, :], words_view(w2_words))
+        nc.sync.dma_start(w23_w_raw[:, 1, :], words_view(w3_words))
         w23_s_raw = keep.tile([P, N], U8, name="w23_s_raw", tag="raw_scales", align_bytes=64)
         nc.vector.memset(w23_s_raw[:].bitcast(I32), 0)
         load_scales([nc.sync] * 4, w23_s_raw, 4, w3_scales)
         load_scales([nc.sync] * 4, w23_s_raw, 0, w2_scales)
+        place_scales(nc.sync, hz_s, hz_s_runs)
 
 
         gain_abs = tile("gain_abs", [P, PACK], F32)
@@ -111,7 +123,7 @@ def tile_picked_mixhgspanfrac_none_po_kernel(
         nc.vector.tensor_scalar(gain_pos[:], gain[:], 0.0, 2.0, ALU.is_ge, ALU.mult)
         nc.vector.tensor_scalar(gain_sign[:], gain_pos[:], -1.0, None, ALU.add)
 
-        y_bank = [psum.tile([P, S], F32, name=f"y_bank{t}", tag=f"bank{t % 3}") for t in range(PACK)]
+        y_bank = [psum.tile([P, S], F32, name=f"y_bank{t}", tag=f"bank{t}") for t in range(PACK)]
 
         def y_product(t):
             cols = slice(t * P, (t + 1) * P)
@@ -139,23 +151,13 @@ def tile_picked_mixhgspanfrac_none_po_kernel(
         def y_out_vector(t):
             nc.vector.tensor_scalar(y_win[t][:, :S], y_bank[t][:], gain_abs[:, t : t + 1], None, ALU.mult)
 
-        hz_w = keep.tile([P, S], I32, name="hz_w", tag="x_s_then_hz_w", align_bytes=64)
-        hz_s_runs = keep.tile([P, S], U8, name="hz_s_runs", tag="pick_s_then_hz_s_runs", align_bytes=64)
-        y_product(0)
-        y_product(1)
-        y_product(2)
+        hz_w = tile("hz_w", [P, S], I32)
+        for t in range(PACK):
+            y_product(t)
         y_out_scalar(0)
         nc.vector.tensor_copy(hz_w[:].bitcast(U32), x_w[:].bitcast(U32).indirect(hz_t[:]))
-        y_out_vector(1)
-        y_out_vector(2)
-        y_product(3)
-        fetch_members(0, 0)
-        fetch_members(0, 1)
-        fetch_members(0, 2)
-        y_out_scalar(3)
-        nc.vector.tensor_copy(hz_s_runs[:], x_s_runs[:].indirect(hz_t[:]))
-        for r in range(4):
-            nc.sync.dma_start(hz_s[r:P:32, :].bitcast(I32), hz_s_runs[8 * r : P : 32, :].bitcast(I32))
+        for t in range(1, PACK):
+            y_out_vector(t)
 
         w23_w = tile("w23_w", [P, 2, N], I32)
         w23_s = tile("w23_s", [P, N], U8)
@@ -172,7 +174,7 @@ def tile_picked_mixhgspanfrac_none_po_kernel(
         h_own = [tile(f"h_own{half}", [P, PACK, S // 2], F32) for half in range(2)]
 
         h_shared = [psum.tile([P, PACK, ZC], F32, name=f"h_bank{b}") for b in range(NZ - 1)]
-        h_last = [psum.tile([P, ZC], F32, name=f"h_last{t}", tag=f"bank{(t + 1) % 4}") for t in range(PACK)]
+        h_last = [psum.tile([P, ZC], F32, name=f"h_last{t}", tag=f"bank{t}") for t in range(PACK)]
 
         def h_sum(b, t):
             return h_last[t][:] if b == NZ - 1 else h_shared[b][:, t, :]
@@ -223,8 +225,7 @@ def tile_picked_mixhgspanfrac_none_po_kernel(
 
         for i in range(len(Z_CHUNKS)):
             for t in range(PACK):
-                if (i, t) not in ((0, 0), (0, 1), (0, 2)):
-                    fetch_members(i, t)
+                fetch_members(i, t)
         for which in range(2):
             deal_words(w23_w[:, which, :], w23_w_raw[:, which, :])
         deal_scales(w23_s[:], w23_s_raw[:])
@@ -237,10 +238,10 @@ def tile_picked_mixhgspanfrac_none_po_kernel(
             pairs(c, 0, lo2, ALU.min)
             if c > 0:
                 sign(c - 1)
-            pairs(c, 1, hi2, ALU.max)
+            pairs(c, 1, lo2, ALU.min)
             if c > 0:
                 quantise_z(c - 1)
-            pairs(c, 1, lo2, ALU.min)
+            pairs(c, 1, hi2, ALU.max)
             finish(c, lo, lo2, ALU.min)
             finish(c, hi, hi2, ALU.max)
         combine(nch - 1)
@@ -253,7 +254,8 @@ def tile_picked_mixhgspanfrac_none_po_kernel(
             nc.sync.dma_start(h_win[t][:, : S // 2], h_own[0][:, t, :])
         for b in range(2, NZ):
             for t in range(PACK):
-                nc.scalar.copy(h_win[t][:, b * ZC : (b + 1) * ZC], h_sum(b, t))
+                copy = nc.vector.tensor_copy if b == NZ - 1 and t % 2 == 0 else nc.scalar.copy
+                copy(h_win[t][:, b * ZC : (b + 1) * ZC], h_sum(b, t))
         for t in range(PACK):
             nc.sync.dma_start(h_own[1][:, t, :], h_win[t][:, S // 2 :])
 

from contextlib import ExitStack

import concourse.mybir as mybir

K, T, S, N, H, W = 512, 2048, 512, 512, 512, 2048
FLOPS = 3 * 2 * 512 * 512 * 512

F32 = mybir.dt.float32
BF16 = mybir.dt.bfloat16
I32 = mybir.dt.int32
U32 = mybir.dt.uint32
U16 = mybir.dt.uint16
U8 = mybir.dt.uint8
FP8X4 = mybir.dt.float8_e4m3fn_x4
ALU = mybir.AluOpType
ACT = mybir.ActivationFunctionType

P = 128
PACK = 4
GROUP = 4
ZC = 128
NZ = S // ZC
SPARE = 16
X_S_VECTOR = 1280
Z_CHUNKS = ((0, 128), (128, 128), (256, 128), (384, 64), (448, 64))
OUT_CHUNKS = ((0, 256), (256, 128), (384, 128))


def words_view(ap):
    return ap[0].rearrange("p n t -> p (n t)").bitcast(I32)


def tile_picked_mixhgspanfrac_none_po_kernel(
    tc, x_words, x_scales, w1_words, w1_scales, gn, w2_words, w2_scales, w3_words, w3_scales, offs, n1, hz, n2, n3, out_0, out_1, out_2
):
    nc = tc.nc
    with ExitStack() as ctx:
        lists = ctx.enter_context(tc.tile_pool(name="lists", bufs=1))
        keep = ctx.enter_context(tc.tile_pool(name="keep", bufs=1))
        psum = ctx.enter_context(tc.psum_pool(name="psum", bufs=1))

        def tile(name, shape, dtype):
            return keep.tile(shape, dtype, name=name, align_bytes=64)

        offs_t = lists.tile([P, S // 16], U16, name="offs_t")
        n1_t = lists.tile([P, W // 16], U16, name="n1_t")
        hz_t = lists.tile([P, S // 16], U16, name="hz_t")
        n2_t = lists.tile([P, S // 16], U16, name="n2_t")
        n3_t = lists.tile([P, S // 16], U16, name="n3_t")

        x_w = tile("x_w", [P, T], I32)
        x_s = tile("x_s", [P, T], U8)
        w1_w_raw = tile("w1_w_raw", [P, H], I32)
        gain = tile("gain", [P, PACK], F32)
        w1_s_raw = keep.tile([P, H], U8, name="w1_s_raw", tag="raw_scales", align_bytes=64)
        pick_s = tile("pick_s", [P, S], U8)
        hz_s = tile("hz_s", [P, S], U8)
        y_win = [tile(f"y_win{t}", [P, S + SPARE], F32) for t in range(PACK)]

        def load_scales(queues, dst, first, src):
            for q, queue in enumerate(queues):
                queue.dma_start(dst[32 * q + first : 32 * q + first + 4, :].bitcast(I32), src[0, 4 * q : 4 * q + 4, :].bitcast(I32))

        def place_scales(queue, dst, src):
            for r in range(4):
                queue.dma_start(dst[r:P:32, :].bitcast(I32), src[8 * r : P : 32, :].bitcast(I32))

        nc.vector.memset(x_s[:, :X_S_VECTOR].bitcast(I32), 0)
        nc.gpsimd.memset(x_s[:, X_S_VECTOR:].bitcast(I32), 0)
        for t in range(PACK):
            nc.gpsimd.memset(y_win[t][:, S:], 0.0)
        nc.gpsimd.dma_start(gain[:], gn.rearrange("(p t) o -> p (t o)", t=PACK))
        nc.vector.memset(w1_s_raw[:].bitcast(I32), 0)
        nc.sync.dma_start(offs_t[:], offs)
        nc.sync.dma_start(w1_w_raw[:], words_view(w1_words))
        nc.sync.dma_start(x_s[0:P:8, :].bitcast(I32), x_scales[0].bitcast(I32))
        nc.sync.dma_start(n1_t[:], n1)
        nc.sync.dma_start(hz_t[:], hz)
        nc.sync.dma_start(n3_t[:], n3)
        nc.sync.dma_start(n2_t[:], n2)
        nc.sync.dma_start(x_w[:], words_view(x_words))
        load_scales([nc.scalar] * 4, w1_s_raw, 0, w1_scales)
        nc.vector.memset(pick_s[:].bitcast(I32), 0)
        nc.vector.memset(hz_s[:].bitcast(I32), 0)

        warm = tile("warm", [P, 1], F32)
        nc.scalar.activation(warm[:], y_win[0][:, S : S + 1], ACT.Abs_reciprocal_sqrt, bias=0.5)

        def deal_words(dst, src):
            nc.vector.tensor_copy(
                dst.rearrange("p (t a i) -> p a t i", t=PACK, i=4),
                src.rearrange("p (a i t) -> p a t i", t=PACK, i=4),
            )

        def deal_scales(dst, src):
            nc.vector.tensor_copy(dst.rearrange("p (t m) -> p t m", t=PACK), src.rearrange("p (m t) -> p t m", t=PACK))

        w1_w = tile("w1_w", [P, H], I32)
        w1_s = tile("w1_s", [P, H], U8)
        deal_words(w1_w[:], w1_w_raw[:])
        pick_s_runs = keep.tile([P, S], U8, name="pick_s_runs", tag="pick_s_runs_then_w23", align_bytes=64)
        nc.vector.tensor_copy(pick_s_runs[:], x_s[:].indirect(offs_t[:]))
        place_scales(nc.scalar, pick_s, pick_s_runs)
        deal_scales(w1_s[:], w1_s_raw[:])
        pick_w = tile("pick_w", [P, S], I32)
        nc.vector.tensor_copy(pick_w[:].bitcast(U32), x_w[:].bitcast(U32).indirect(offs_t[:]))
        hz_s_runs = tile("hz_s_runs", [P, S], U8)
        nc.vector.tensor_copy(hz_s_runs[:], x_s[:].indirect(hz_t[:]))
        w23_w_raw = keep.tile([P, 2, N], I32, name="w23_w_raw", tag="pick_s_runs_then_w23", align_bytes=64)
        nc.sync.dma_start(w23_w_raw[:, 0, :], words_view(w2_words))
        nc.sync.dma_start(w23_w_raw[:, 1, :], words_view(w3_words))
        w23_s_raw = keep.tile([P, N], U8, name="w23_s_raw", tag="raw_scales", align_bytes=64)
        nc.vector.memset(w23_s_raw[:].bitcast(I32), 0)
        load_scales([nc.sync] * 4, w23_s_raw, 4, w3_scales)
        load_scales([nc.sync] * 4, w23_s_raw, 0, w2_scales)
        place_scales(nc.sync, hz_s, hz_s_runs)


        gain_abs = tile("gain_abs", [P, PACK], F32)
        gain_pos = tile("gain_pos", [P, PACK], F32)
        gain_sign = tile("gain_sign", [P, PACK], BF16)
        nc.vector.scalar_tensor_tensor(gain_abs[:], gain[:], -1.0, gain[:], ALU.mult, ALU.max)
        nc.vector.tensor_scalar(gain_pos[:], gain[:], 0.0, 2.0, ALU.is_ge, ALU.mult)
        nc.vector.tensor_scalar(gain_sign[:], gain_pos[:], -1.0, None, ALU.add)

        y_bank = [psum.tile([P, S], F32, name=f"y_bank{t}", tag=f"bank{t}") for t in range(PACK)]

        def y_product(t):
            cols = slice(t * P, (t + 1) * P)
            nc.tensor.matmul_mx(
                out=y_bank[t][:],
                lhsT=w1_w[:, cols].bitcast(FP8X4),
                lhsT_scale=w1_s[:, cols],
                rhs=pick_w[:].bitcast(FP8X4),
                rhs_scale=pick_s[:],
                start=True,
                stop=True,
            )

        nch = len(Z_CHUNKS)
        members = [tile(f"members{c}", [P, PACK, w * GROUP], F32) for c, (c0, w) in enumerate(Z_CHUNKS)]

        def fetch_members(c, t):
            c0, w = Z_CHUNKS[c]
            entries = n1_t[:, c0 * GROUP // 16 : (c0 + w) * GROUP // 16]
            nc.scalar.activation(members[c][:, t, :], y_win[t][:].indirect(entries), ACT.Copy)

        def y_out_scalar(t):
            nc.scalar.activation(y_win[t][:, :S], y_bank[t][:], ACT.Copy, scale=gain_abs[:, t : t + 1])

        def y_out_vector(t):
            nc.vector.tensor_scalar(y_win[t][:, :S], y_bank[t][:], gain_abs[:, t : t + 1], None, ALU.mult)

        hz_w = tile("hz_w", [P, S], I32)
        for t in range(PACK):
            y_product(t)
        y_out_scalar(0)
        nc.vector.tensor_copy(hz_w[:].bitcast(U32), x_w[:].bitcast(U32).indirect(hz_t[:]))
        for t in range(1, PACK):
            y_out_vector(t)

        w23_w = tile("w23_w", [P, 2, N], I32)
        w23_s = tile("w23_s", [P, N], U8)

        hi2 = [tile(f"hi2_{c}", [P, w, PACK, 2], F32) for c, (c0, w) in enumerate(Z_CHUNKS)]
        lo2 = [tile(f"lo2_{c}", [P, w, PACK, 2], F32) for c, (c0, w) in enumerate(Z_CHUNKS)]
        hi = [tile(f"hi_{c}", [P, w, PACK], F32) for c, (c0, w) in enumerate(Z_CHUNKS)]
        lo = [tile(f"lo_{c}", [P, w, PACK], F32) for c, (c0, w) in enumerate(Z_CHUNKS)]
        z_abs = [tile(f"z_abs{c}", [P, w, PACK], BF16) for c, (c0, w) in enumerate(Z_CHUNKS)]
        z = [tile(f"z{c}", [P, w, PACK], BF16) for c, (c0, w) in enumerate(Z_CHUNKS)]
        z_w = tile("z_w", [P, S], I32)
        z_s = tile("z_s", [P, S], U8)
        h_win = [tile(f"h_win{t}", [P, S], F32) for t in range(PACK)]
        h_own = [tile(f"h_own{half}", [P, PACK, S // 2], F32) for half in range(2)]

        h_shared = [psum.tile([P, PACK, ZC], F32, name=f"h_bank{b}") for b in range(NZ - 1)]
        h_last = [psum.tile([P, ZC], F32, name=f"h_last{t}", tag=f"bank{t}") for t in range(PACK)]

        def h_sum(b, t):
            return h_last[t][:] if b == NZ - 1 else h_shared[b][:, t, :]

        def pairs(c, u, dst, op):
            m = members[c][:, 2 * u : 2 * u + 2, :].rearrange("p t (j g) -> p j t g", g=GROUP)
            nc.vector.tensor_tensor(dst[c][:, :, 2 * u : 2 * u + 2, :], m[:, :, :, 0:2], m[:, :, :, 2:4], op)

        def finish(c, dst, src, op):
            nc.vector.tensor_tensor(dst[c][:], src[c][:, :, :, 0], src[c][:, :, :, 1], op)

        def combine(c):
            nc.vector.scalar_tensor_tensor(
                z_abs[c][:].rearrange("p j t -> p (j t)"),
                lo[c][:].rearrange("p j t -> p (j t)"),
                -0.5,
                hi[c][:].rearrange("p j t -> p (j t)"),
                ALU.mult,
                ALU.add,
            )

        def sign(c):
            w = Z_CHUNKS[c][1]
            nc.vector.tensor_tensor(z[c][:], z_abs[c][:], gain_sign[:].unsqueeze(1).to_broadcast([P, w, PACK]), ALU.mult)

        def h_pass(b, which, rhs, rhs_scale):
            cols = slice(b * ZC, (b + 1) * ZC)
            alone = b == NZ - 1
            for t in range(PACK):
                rows = slice(t * P, (t + 1) * P)
                nc.tensor.matmul_mx(
                    out=h_sum(b, t),
                    lhsT=w23_w[:, which, rows].bitcast(FP8X4),
                    lhsT_scale=w23_s[4 * which : P, rows],
                    rhs=rhs[:, cols].bitcast(FP8X4),
                    rhs_scale=rhs_scale[:, cols],
                    start=(which == 1 and (alone or t == 0)),
                    stop=(which == 0 and (alone or t == PACK - 1)),
                )

        def quantise_z(c):
            c0, w = Z_CHUNKS[c]
            nc.vector.quantize_mx(
                out=z_w[:, c0 : c0 + w].bitcast(FP8X4), scales=z_s[:, c0 : c0 + w], in_=z[c][:].rearrange("p j t -> p (j t)")
            )
            if (c0 + w) % ZC == 0:
                h_pass(c0 // ZC, 0, z_w, z_s)

        for i in range(len(Z_CHUNKS)):
            for t in range(PACK):
                fetch_members(i, t)
        for which in range(2):
            deal_words(w23_w[:, which, :], w23_w_raw[:, which, :])
        deal_scales(w23_s[:], w23_s_raw[:])
        for b in range(NZ):
            h_pass(b, 1, hz_w, hz_s)
        for c in range(nch):
            pairs(c, 0, hi2, ALU.max)
            if c > 0:
                combine(c - 1)
            pairs(c, 0, lo2, ALU.min)
            if c > 0:
                sign(c - 1)
            pairs(c, 1, lo2, ALU.min)
            if c > 0:
                quantise_z(c - 1)
            pairs(c, 1, hi2, ALU.max)
            finish(c, lo, lo2, ALU.min)
            finish(c, hi, hi2, ALU.max)
        combine(nch - 1)
        sign(nch - 1)
        quantise_z(nch - 1)

        for b in range(2):
            nc.scalar.copy(h_own[0][:, :, b * ZC : (b + 1) * ZC], h_shared[b][:])
        for t in range(PACK):
            nc.sync.dma_start(h_win[t][:, : S // 2], h_own[0][:, t, :])
        for b in range(2, NZ):
            for t in range(PACK):
                copy = nc.vector.tensor_copy if b == NZ - 1 and t % 2 == 0 else nc.scalar.copy
                copy(h_win[t][:, b * ZC : (b + 1) * ZC], h_sum(b, t))
        for t in range(PACK):
            nc.sync.dma_start(h_own[1][:, t, :], h_win[t][:, S // 2 :])

        def own(c0, w):
            return h_own[c0 // (S // 2)][:, :, c0 % (S // 2) : c0 % (S // 2) + w]

        out_rows = out_0.rearrange("(p t) c -> p t c", t=PACK)
        out_w = tile("out_w", [P, S], I32)
        out_s = tile("out_s", [P, S], U8)

        def per_chunk(name):
            return [tile(f"{name}{k}", [P, PACK, w], F32) for k, (c0, w) in enumerate(OUT_CHUNKS)]

        diff, dist, root, inv, res = (per_chunk(name) for name in ("diff", "dist", "root", "inv", "res"))
        other = tile("other", [P, PACK, S // 2], F32)
        neg_num = [tile(f"neg_num{half}", [P, PACK, S // 2], F32) for half in range(2)]
        res_b = [tile(f"res_b{k}", [P, w, PACK], BF16) for k, (c0, w) in enumerate(OUT_CHUNKS)]

        def halves(k):
            return (slice(0, 2), slice(2, 4)) if k == 0 else (slice(0, 4),)

        def fetch_less_own(dst, list_t, c0, w):
            for t in range(PACK):
                nc.vector.tensor_tensor(
                    dst[:, t, :], h_win[t][:].indirect(list_t[:, c0 // 16 : (c0 + w) // 16]), own(c0, w)[:, t, :], ALU.subtract
                )

        def fetch_other():
            for t in range(PACK):
                nc.scalar.activation(other[:, t, :], h_win[t][:].indirect(n3_t[:, S // 32 :]), ACT.Copy)

        def less_own(k):
            c0, w = OUT_CHUNKS[k]
            nc.vector.tensor_tensor(diff[k][:], other[:, :, c0 - S // 2 : c0 - S // 2 + w], own(c0, w), ALU.subtract)

        def denominators(k):
            for ts in halves(k):
                nc.scalar.activation(dist[k][:, ts, :], diff[k][:, ts, :], ACT.Abs)
                nc.scalar.activation(root[k][:, ts, :], dist[k][:, ts, :], ACT.Abs_reciprocal_sqrt, bias=0.5)
                nc.scalar.activation(inv[k][:, ts, :], root[k][:, ts, :], ACT.Square)

        def quotient(k):
            c0, w = OUT_CHUNKS[k]
            for ts in halves(k):
                nc.vector.scalar_tensor_tensor(res[k][:, ts, :], neg_num[c0 // (S // 2)][:, ts, c0 % (S // 2) : c0 % (S // 2) + w], -1.0, inv[k][:, ts, :], ALU.mult, ALU.mult)
                nc.sync.dma_start(out_rows[:, ts, c0 : c0 + w], res[k][:, ts, :])

        def interleave(k, copy):
            copy(res_b[k][:].rearrange("p (a i) t -> p a t i", i=4), res[k][:].rearrange("p t (a i) -> p a t i", i=4))

        def quantise_out(k):
            c0, w = OUT_CHUNKS[k]
            nc.vector.quantize_mx(
                out=out_w[:, c0 : c0 + w].bitcast(FP8X4), scales=out_s[:, c0 : c0 + w], in_=res_b[k][:].rearrange("p j t -> p (j t)")
            )
            nc.sync.dma_start(words_view(out_1)[:, c0 : c0 + w], out_w[:, c0 : c0 + w])

        fetch_less_own(diff[0], n3_t, *OUT_CHUNKS[0])
        fetch_other()
        denominators(0)
        less_own(1)
        less_own(2)
        denominators(1)
        denominators(2)
        fetch_less_own(neg_num[0], n2_t, 0, S // 2)
        quotient(0)
        interleave(0, nc.scalar.copy)
        fetch_less_own(neg_num[1], n2_t, S // 2, S // 2)
        quotient(1)
        interleave(1, nc.scalar.copy)
        quotient(2)
        quantise_out(0)
        interleave(2, nc.vector.tensor_copy)
        quantise_out(1)
        quantise_out(2)
        for q in range(4):
            queue = nc.scalar if q % 2 else nc.sync
            queue.dma_start(out_2[0, 4 * q : 4 * q + 4, :].bitcast(I32), out_s[32 * q : 32 * q + 4, :].bitcast(I32))
